import numpy as np
import ml_dtypes


def mxq(x, axis, fmt="e4m3"):
    dtype, down = {"e4m3": (ml_dtypes.float8_e4m3fn, 7), "e5m2": (ml_dtypes.float8_e5m2, 14)}[fmt]
    v = np.moveaxis(np.asarray(x, np.float32).astype(ml_dtypes.bfloat16).astype(np.float64), axis, -1)
    blocks = v.reshape(v.shape[:-1] + (-1, 32))
    amax = np.abs(blocks).max(-1, keepdims=True)
    byte = np.maximum(np.where(amax > 0, np.frexp(amax)[1] - 1 + 127, 0) - down, 1)
    scale = np.exp2(byte - 127.0)
    codes = (blocks / scale).astype(np.float32).astype(dtype).astype(np.float64)
    return np.moveaxis((codes * scale).reshape(v.shape), -1, axis)


WIDE = False


def mx_kscale(k):
    if not WIDE:
        return np.ones(k)
    levels = np.array([10, -10, 5, -5, 0])
    if k % 512:
        return np.exp2(np.random.permutation(np.resize(levels, k // 32))).repeat(32)
    a = np.empty((k // 512, 16))
    for p in range(k // 512):
        a[p, :8] = np.random.permutation(np.resize(levels, 8))
        for g in range(8):
            far = levels[np.abs(levels - a[p, g]) >= 10]
            a[p, g + 8] = far[np.random.randint(len(far))]
    return np.exp2(a.ravel()).repeat(32)


def f64(x):
    return np.asarray(x).astype(np.float64)


def striped8(idx):
    return np.asarray(idx).reshape(8, -1, 16).transpose(0, 2, 1).reshape(128, -1).astype(np.uint16)


def unstriped8(offs):
    return offs.reshape(8, 16, -1).transpose(0, 2, 1).reshape(8, -1).astype(np.int64)


def pick8(x, idx, run):
    r = np.arange(len(x))
    return x[r[:, None], idx[r % (8 * run) // run]]


E2M1 = np.array([0.0, 0.5, 1.0, 1.5, 2.0, 3.0, 4.0, 6.0, -0.0, -0.5, -1.0, -1.5, -2.0, -3.0, -4.0, -6.0])


def pack_weight(w, fmt):
    k, n = w.shape
    w = f64(np.asarray(w, np.float32).astype(ml_dtypes.bfloat16)).reshape(k // 32, 32, n)
    amax = np.abs(w).max(1)
    if fmt == "e4m3":
        byte = np.frexp(amax)[1] - 1 + 127 - 7
    else:
        mant, ex = np.frexp(amax / 6.0)
        byte = np.where(mant > 0.5, ex, ex - 1) + 127
    byte = np.clip(np.where(amax > 0, byte, 1), 1, 254)
    scaled = (w * np.exp2(127.0 - byte)[:, None, :]).reshape(k, n).astype(np.float32)
    by_word = np.ascontiguousarray(scaled.reshape(k // 512, 128, 4, n).transpose(0, 1, 3, 2))
    if fmt == "e4m3":
        words = by_word.astype(ml_dtypes.float8_e4m3fn).view(np.uint8)
    else:
        c = by_word.astype(ml_dtypes.float4_e2m1fn).view(np.uint8) & 0xF
        words = (c[..., 0::2] | (c[..., 1::2] << 4)).reshape(k // 512, 128, 2 * n)
    return np.ascontiguousarray(words), np.ascontiguousarray(byte.astype(np.uint8).reshape(k // 512, 16, n))


def unpack_weight(words, scales, fmt):
    g, _, n = scales.shape
    words = np.ascontiguousarray(words).reshape(g, 128, n, -1)
    if fmt == "e4m3":
        vals = words.view(ml_dtypes.float8_e4m3fn).astype(np.float64)
    else:
        nib = np.empty((g, 128, n, 4), np.uint8)
        nib[..., 0::2] = words & 0xF
        nib[..., 1::2] = words >> 4
        vals = E2M1[nib]
    vals = vals * np.repeat(np.exp2(scales.astype(np.float64) - 127.0), 8, axis=1)[..., None]
    return vals.transpose(0, 1, 3, 2).reshape(g * 512, n)


D, T, I, Q, E = 512, 1024, 512, 512, 256


def setup_inputs():
    n = np.random.standard_normal
    idx = np.stack([np.random.permutation(T)[:I] for _ in range(8)])
    idx2 = np.stack([np.random.permutation(T)[:I] for _ in range(8)])
    idx3 = np.stack([np.random.permutation(T)[:I] for _ in range(8)])
    idx4 = np.stack([np.random.permutation(T)[:I] for _ in range(8)])
    idx5 = np.stack([np.random.permutation(T)[:I] for _ in range(8)])
    idx6 = np.stack([np.random.permutation(T)[:I] for _ in range(8)])
    fd = mx_kscale(D)
    fq = mx_kscale(Q)
    keysp = pack_weight(n((D, T)) / fd[:, None], "e4m3")
    mixp = pack_weight(n((Q, E)) * 1.0 / np.sqrt(Q) / fq[:, None], "e2m1")
    return {
        "query": (n((D, Q)) * 1.0 / np.sqrt(D) * fd[:, None]).astype(np.float32),
        "keys_words": keysp[0],
        "keys_scales": keysp[1],
        "rowf": (np.random.uniform(0.5, 2.0, (Q, 1)) * fq[:, None]).astype(np.float32),
        "mix_words": mixp[0],
        "mix_scales": mixp[1],
        "offs": striped8(idx),
        "offs2": striped8(idx2),
        "offs3": striped8(idx3),
        "offs4": striped8(idx4),
        "offs5": striped8(idx5),
        "offs6": striped8(idx6),
    }


def reference(query, keys_words, keys_scales, rowf, mix_words, mix_scales, offs, offs2, offs3, offs4, offs5, offs6):
    idx = unstriped8(offs)
    idx2 = unstriped8(offs2)
    idx3 = unstriped8(offs3)
    idx4 = unstriped8(offs4)
    idx5 = unstriped8(offs5)
    idx6 = unstriped8(offs6)
    keysu = unpack_weight(keys_words, keys_scales, "e4m3")
    mixu = unpack_weight(mix_words, mix_scales, "e2m1")
    queryq = mxq(f64(query), 0, "e4m3")
    a = queryq.T @ keysu
    hi1 = np.maximum(pick8(a, idx, 64), pick8(a, idx2, 64))
    lo1 = np.minimum(pick8(a, idx3, 64), pick8(a, idx4, 64))
    r = hi1 - lo1
    f1 = np.zeros((Q, T))
    f1[np.arange(Q)[:, None], idx5[np.arange(Q) % 512 // 64]] = r
    c1 = a - f1
    g = pick8(c1, idx6, 64) + lo1
    gw = g * f64(rowf)
    gwq = mxq(gw, 0, "e4m3")
    y = mixu.T @ gwq
    return y

@@ -1,0 +1,207 @@
+from contextlib import ExitStack
+
+import concourse.mybir as mybir
+
+D, T, I, Q, E = 512, 1024, 512, 512, 256
+FLOPS = 2 * D * Q * T + 2 * Q * E * I
+
+F32 = mybir.dt.float32
+BF16 = mybir.dt.bfloat16
+I32 = mybir.dt.int32
+U32 = mybir.dt.uint32
+U16 = mybir.dt.uint16
+U8 = mybir.dt.uint8
+FP8X4 = mybir.dt.float8_e4m3fn_x4
+FP4X4 = mybir.dt.float4_e2m1fn_x4
+ALU = mybir.AluOpType
+COPY = mybir.ActivationFunctionType.Copy
+
+P = 128
+PACK = 4
+BANK = 512
+HALF = I // 2
+
+
+def tile_attend_spanpassed_one_mixed_kernel(
+    tc, query, keys_words, keys_scales, rowf, mix_words, mix_scales, offs, offs2, offs3, offs4, offs5, offs6, out
+):
+    nc = tc.nc
+    with ExitStack() as ctx:
+        sb = ctx.enter_context(tc.tile_pool(name="sb", bufs=1))
+        ps = ctx.enter_context(tc.psum_pool(name="ps", bufs=1))
+
+        key_scale = sb.tile([P, T], U8, name="key_scale", align_bytes=64)
+        mix_scale = sb.tile([P, E], U8, name="mix_scale", align_bytes=64)
+        nc.vector.memset(key_scale[:].bitcast(I32), 0)
+        nc.vector.memset(mix_scale[:].bitcast(I32), 0)
+
+        q_rows = query.rearrange("(p j) q -> p j q", j=PACK)
+        q_raw = []
+        for h in range(2):
+            raw = sb.tile([P, PACK, Q // 2], F32, name=f"q_raw{h}")
+            nc.sync.dma_start(out=raw[:], in_=q_rows[:, :, h * (Q // 2) : (h + 1) * (Q // 2)])
+            q_raw.append(raw)
+        key_src = keys_words[0].rearrange("p n t -> p (n t)").bitcast(I32)
+        key_words = []
+        for b in range(T // BANK):
+            words = sb.tile([P, BANK], I32, name=f"key_words{b}", align_bytes=64)
+            nc.sync.dma_start(out=words[:], in_=key_src[:, b * BANK : (b + 1) * BANK])
+            key_words.append(words)
+        for quad in range(4):
+            nc.sync.dma_start(
+                out=key_scale[32 * quad : 32 * quad + 4, :].bitcast(I32),
+                in_=keys_scales[0, 4 * quad : 4 * quad + 4, :].bitcast(I32),
+            )
+        lists = {}
+        for name, src in (("hi_a", offs), ("lo_a", offs3), ("hi_b", offs2), ("lo_b", offs4), ("put", offs5), ("get", offs6)):
+            lists[name] = sb.tile([P, I // 16], U16, name=f"list_{name}")
+            nc.sync.dma_start(lists[name][:], src)
+        row_factor = sb.tile([P, PACK], F32, name="row_factor")
+        nc.sync.dma_start(out=row_factor[:], in_=rowf.rearrange("(p t) o -> p (t o)", t=PACK))
+        mix_codes = sb.tile([P, 2 * E], U8, name="mix_codes", align_bytes=64)
+        nc.sync.dma_start(out=mix_codes[:].bitcast(I32), in_=mix_words[0].bitcast(I32))
+        for quad in range(4):
+            nc.sync.dma_start(
+                out=mix_scale[32 * quad : 32 * quad + 4, :].bitcast(I32),
+                in_=mix_scales[0, 4 * quad : 4 * quad + 4, :].bitcast(I32),
+            )
+
+        span_at = sb.tile([P, T], F32, name="span_at")
+        nc.vector.memset(span_at[:], 0.0)
+
+        q_first = sb.tile([P, P, PACK], BF16, name="q_first", align_bytes=64)
+        q_rest = sb.tile([P, PACK - 1, P, PACK], BF16, name="q_rest", align_bytes=64)
+        for h in range(2):
+            cols = slice(h * (P // 2), (h + 1) * (P // 2))
+            dealt = q_raw[h][:].rearrange("p j (m t) -> p m t j", t=PACK)
+            nc.vector.tensor_copy(out=q_first[:, cols, :], in_=dealt[:, :, 0, :])
+            nc.scalar.activation(
+                out=q_rest[:, :, cols, :].rearrange("p t m j -> p m t j"), in_=dealt[:, :, 1:PACK, :], func=COPY
+            )
+        q_codes, q_scale = [], []
+        for t in range(PACK):
+            codes = sb.tile([P, P], U32, name=f"q_codes{t}", align_bytes=64)
+            scale = sb.tile([P, P], U8, name=f"q_scale{t}", align_bytes=64)
+            src = q_first[:] if t == 0 else q_rest[:, t - 1, :, :]
+            nc.vector.quantize_mx(out=codes[:].bitcast(FP8X4), scales=scale[:], in_=src.rearrange("p m j -> p (m j)"))
+            q_codes.append(codes)
+            q_scale.append(scale)
+
+        score = [sb.tile([P, T], F32, name=f"score{t}") for t in range(PACK)]
+        first = [sb.tile([P, 2, I], F32, name=f"first{t}") for t in range(PACK)]
+        second = [sb.tile([P, 2, I], F32, name=f"second{t}") for t in range(PACK)]
+        ends = [sb.tile([P, 2, I], F32, name=f"ends{t}") for t in range(PACK)]
+        left = [sb.tile([P, T], F32, name=f"left{t}") for t in range(PACK)]
+        picked = [sb.tile([P, I], F32, name=f"picked{t}") for t in range(PACK - 1)]
+        result = [sb.tile([P, I], F32, name=f"result{t}") for t in range(PACK - 1)]
+        last_result = [sb.tile([P, HALF], F32, name=f"last_result{h}") for h in range(2)]
+        weighted = [sb.tile([P, HALF, PACK], BF16, name=f"weighted{h}", align_bytes=64) for h in range(2)]
+
+        def scores(t):
+            for b in range(T // BANK):
+                cols = slice(b * BANK, (b + 1) * BANK)
+                acc = ps.tile([P, BANK], F32, name=f"acc{t}_{b}", tag=f"score_bank{(2 * t + b) % 4}")
+                nc.tensor.matmul_mx(
+                    out=acc[:],
+                    lhsT=q_codes[t][:].bitcast(FP8X4),
+                    lhsT_scale=q_scale[t][:],
+                    rhs=key_words[b][:].bitcast(FP8X4),
+                    rhs_scale=key_scale[:, cols],
+                    start=True,
+                    stop=True,
+                )
+                if t == 0 and b == 0:
+                    nc.vector.tensor_copy(out=score[t][:, cols], in_=acc[:])
+                else:
+                    nc.scalar.activation(out=score[t][:, cols], in_=acc[:], func=COPY)
+
+        def look_up(t):
+            for dst, hi, lo in ((first[t], "hi_a", "lo_a"), (second[t], "hi_b", "lo_b")):
+                if t == 0:
+                    nc.vector.tensor_copy(out=dst[:, 0, :], in_=score[t][:].indirect(lists[hi][:]))
+                else:
+                    nc.scalar.activation(out=dst[:, 0, :], in_=score[t][:].indirect(lists[hi][:]), func=COPY)
+                nc.scalar.activation(out=dst[:, 1, :], in_=score[t][:].indirect(lists[lo][:]), func=COPY, scale=-1.0)
+
+        def span(t):
+            nc.vector.tensor_tensor(out=ends[t][:], in0=first[t][:], in1=second[t][:], op=ALU.max)
+            nc.vector.tensor_tensor(
+                out=span_at[:].indirect(lists["put"][:]), in0=ends[t][:, 0, :], in1=ends[t][:, 1, :], op=ALU.add
+            )
+
+        def take_off(t):
+            nc.vector.tensor_tensor(out=left[t][:], in0=score[t][:], in1=span_at[:], op=ALU.subtract)
+
+        def pick(t):
+            nc.scalar.activation(out=picked[t][:], in_=left[t][:].indirect(lists["get"][:]), func=COPY)
+
+        def add_low(t):
+            nc.vector.tensor_tensor(out=result[t][:], in0=picked[t][:], in1=ends[t][:, 1, :], op=ALU.subtract)
+
+        def weigh(t, h, src):
+            nc.scalar.activation(out=weighted[h][:, :, t], in_=src, func=COPY, scale=row_factor[:, t : t + 1])
+
+        def weigh_both(t):
+            for h in range(2):
+                weigh(t, h, result[t][:, h * HALF : (h + 1) * HALF])
+
+        scores(0)
+        look_up(0)
+        span(0)
+        take_off(0)
+        scores(1)
+        look_up(1)
+        span(1)
+        take_off(1)
+        scores(2)
+        look_up(2)
+        pick(0)
+        span(2)
+        take_off(2)
+        add_low(0)
+        scores(3)
+        look_up(3)
+        pick(1)
+        add_low(1)
+        span(3)
+        pick(2)
+        weigh_both(0)
+        weigh_both(1)
+        add_low(2)
+        take_off(3)
+        weigh_both(2)
+
+        last = PACK - 1
+        for h in range(2):
+            nc.vector.tensor_tensor(
+                out=last_result[h][:],
+                in0=left[last][:].indirect(lists["get"][:, h * (HALF // 16) : (h + 1) * (HALF // 16)]),
+                in1=ends[last][:, 1, h * HALF : (h + 1) * HALF],
+                op=ALU.subtract,
+            )
+            weigh(last, h, last_result[h][:])
+        for h in range(2):
+            codes = sb.tile([P, HALF], U32, name=f"w_codes{h}", align_bytes=64)
+            scale = sb.tile([P, HALF], U8, name=f"w_scale{h}", align_bytes=64)
+            nc.vector.quantize_mx(
+                out=codes[:].bitcast(FP8X4), scales=scale[:], in_=weighted[h][:].rearrange("p i t -> p (i t)")
+            )
+            for c in range(E // P):
+                acc = ps.tile([P, HALF], F32, name=f"mixed{h}_{c}")
+                nc.tensor.matmul_mx(
+                    out=acc[:],
+                    lhsT=mix_codes[:, 2 * P * c : 2 * P * (c + 1)].bitcast(FP4X4),
+                    lhsT_scale=mix_scale[:, P * c : P * (c + 1)],
+                    rhs=codes[:].bitcast(FP8X4),
+                    rhs_scale=scale[:],
+                    start=True,
+                    stop=True,
+                )
+                staged = sb.tile([P, HALF], F32, name=f"staged{h}_{c}")
+                rows_out = out[P * c : P * (c + 1), h * HALF : (h + 1) * HALF]
+                if c == 0:
+                    nc.vector.tensor_copy(out=staged[:], in_=acc[:])
+                    nc.sync.dma_start(out=rows_out, in_=staged[:])
+                else:
+                    nc.scalar.activation(out=staged[:], in_=acc[:], func=COPY)
+                    nc.scalar.dma_start(out=rows_out, in_=staged[:])

@@ -29,6 +29,7 @@ def tile_attend_spanpassed_one_mixed_kernel(
     with ExitStack() as ctx:
         sb = ctx.enter_context(tc.tile_pool(name="sb", bufs=1))
         ps = ctx.enter_context(tc.psum_pool(name="ps", bufs=1))
+        score_ps = ctx.enter_context(tc.psum_pool(name="score_ps", bufs=1))
 
         key_scale = sb.tile([P, T], U8, name="key_scale", align_bytes=64)
         mix_scale = sb.tile([P, E], U8, name="mix_scale", align_bytes=64)
@@ -41,19 +42,20 @@ def tile_attend_spanpassed_one_mixed_kernel(
             raw = sb.tile([P, PACK, Q // 2], F32, name=f"q_raw{h}")
             nc.sync.dma_start(out=raw[:], in_=q_rows[:, :, h * (Q // 2) : (h + 1) * (Q // 2)])
             q_raw.append(raw)
+            if h == 0:
+                for quad in range(4):
+                    nc.sync.dma_start(
+                        out=key_scale[32 * quad : 32 * quad + 4, :].bitcast(I32),
+                        in_=keys_scales[0, 4 * quad : 4 * quad + 4, :].bitcast(I32),
+                    )
         key_src = keys_words[0].rearrange("p n t -> p (n t)").bitcast(I32)
         key_words = []
         for b in range(T // BANK):
             words = sb.tile([P, BANK], I32, name=f"key_words{b}", align_bytes=64)
             nc.sync.dma_start(out=words[:], in_=key_src[:, b * BANK : (b + 1) * BANK])
             key_words.append(words)
-        for quad in range(4):
-            nc.sync.dma_start(
-                out=key_scale[32 * quad : 32 * quad + 4, :].bitcast(I32),
-                in_=keys_scales[0, 4 * quad : 4 * quad + 4, :].bitcast(I32),
-            )
         lists = {}
-        for name, src in (("hi_a", offs), ("lo_a", offs3), ("hi_b", offs2), ("lo_b", offs4), ("put", offs5), ("get", offs6)):
+        for name, src in (("lo_a", offs3), ("hi_a", offs), ("lo_b", offs4), ("hi_b", offs2), ("put", offs5), ("get", offs6)):
             lists[name] = sb.tile([P, I // 16], U16, name=f"list_{name}")
             nc.sync.dma_start(lists[name][:], src)
         row_factor = sb.tile([P, PACK], F32, name="row_factor")
@@ -75,34 +77,41 @@ def tile_attend_spanpassed_one_mixed_kernel(
             cols = slice(h * (P // 2), (h + 1) * (P // 2))
             dealt = q_raw[h][:].rearrange("p j (m t) -> p m t j", t=PACK)
             nc.vector.tensor_copy(out=q_first[:, cols, :], in_=dealt[:, :, 0, :])
-            nc.scalar.activation(
-                out=q_rest[:, :, cols, :].rearrange("p t m j -> p m t j"), in_=dealt[:, :, 1:PACK, :], func=COPY
-            )
-        q_codes, q_scale = [], []
-        for t in range(PACK):
-            codes = sb.tile([P, P], U32, name=f"q_codes{t}", align_bytes=64)
-            scale = sb.tile([P, P], U8, name=f"q_scale{t}", align_bytes=64)
+            rest = q_rest[:, :, cols, :].rearrange("p t m j -> p m t j")
+            if h == 0:
+                nc.vector.tensor_copy(out=rest, in_=dealt[:, :, 1:PACK, :])
+            else:
+                nc.scalar.activation(out=rest, in_=dealt[:, :, 1:PACK, :], func=COPY)
+        q_codes = [sb.tile([P, P], U32, name=f"q_codes{t}", align_bytes=64) for t in range(PACK)]
+        q_scale = [sb.tile([P, P], U8, name=f"q_scale{t}", align_bytes=64) for t in range(PACK)]
+
+        def quantise_query(t):
             src = q_first[:] if t == 0 else q_rest[:, t - 1, :, :]
-            nc.vector.quantize_mx(out=codes[:].bitcast(FP8X4), scales=scale[:], in_=src.rearrange("p m j -> p (m j)"))
-            q_codes.append(codes)
-            q_scale.append(scale)
+            nc.vector.quantize_mx(
+                out=q_codes[t][:].bitcast(FP8X4), scales=q_scale[t][:], in_=src.rearrange("p m j -> p (m j)")
+            )
 
         score = [sb.tile([P, T], F32, name=f"score{t}") for t in range(PACK)]
         first = [sb.tile([P, 2, I], F32, name=f"first{t}") for t in range(PACK)]
         second = [sb.tile([P, 2, I], F32, name=f"second{t}") for t in range(PACK)]
         ends = [sb.tile([P, 2, I], F32, name=f"ends{t}") for t in range(PACK)]
         left = [sb.tile([P, T], F32, name=f"left{t}") for t in range(PACK)]
-        picked = [sb.tile([P, I], F32, name=f"picked{t}") for t in range(PACK - 1)]
         result = [sb.tile([P, I], F32, name=f"result{t}") for t in range(PACK - 1)]
         last_result = [sb.tile([P, HALF], F32, name=f"last_result{h}") for h in range(2)]
-        weighted = [sb.tile([P, HALF, PACK], BF16, name=f"weighted{h}", align_bytes=64) for h in range(2)]
+        pairs = [sb.tile([P, 2, HALF, 2], BF16, name=f"pairs{h}") for h in range(2)]
+        weighted = [sb.tile([P, HALF * PACK], BF16, name=f"weighted{h}", align_bytes=64) for h in range(2)]
+        picked = [ends[2][:, 0, :], first[3][:, 0, :], second[3][:, 0, :]]
 
-        def scores(t):
+        def multiply(t):
+            if t == 0:
+                acc = [score_ps.tile([P, BANK], F32, name=f"first_acc{b}", offset=4 * BANK * b)[:] for b in range(T // BANK)]
+            else:
+                both = score_ps.tile([P, T], F32, name=f"acc{t}", tag="acc", offset=0)
+                acc = [both[:, b * BANK : (b + 1) * BANK] for b in range(T // BANK)]
             for b in range(T // BANK):
                 cols = slice(b * BANK, (b + 1) * BANK)
-                acc = ps.tile([P, BANK], F32, name=f"acc{t}_{b}", tag=f"score_bank{(2 * t + b) % 4}")
                 nc.tensor.matmul_mx(
-                    out=acc[:],
+                    out=acc[b],
                     lhsT=q_codes[t][:].bitcast(FP8X4),
                     lhsT_scale=q_scale[t][:],
                     rhs=key_words[b][:].bitcast(FP8X4),
@@ -110,21 +119,27 @@ def tile_attend_spanpassed_one_mixed_kernel(
                     start=True,
                     stop=True,
                 )
-                if t == 0 and b == 0:
-                    nc.vector.tensor_copy(out=score[t][:, cols], in_=acc[:])
-                else:
-                    nc.scalar.activation(out=score[t][:, cols], in_=acc[:], func=COPY)
+            return acc
 
-        def look_up(t):
-            for dst, hi, lo in ((first[t], "hi_a", "lo_a"), (second[t], "hi_b", "lo_b")):
-                if t == 0:
-                    nc.vector.tensor_copy(out=dst[:, 0, :], in_=score[t][:].indirect(lists[hi][:]))
+        def empty(t, acc):
+            for b in range(T // BANK):
+                cols = slice(b * BANK, (b + 1) * BANK)
+                if t == 0 and b == 1:
+                    nc.vector.tensor_copy(out=score[t][:, cols], in_=acc[b])
                 else:
-                    nc.scalar.activation(out=dst[:, 0, :], in_=score[t][:].indirect(lists[hi][:]), func=COPY)
-                nc.scalar.activation(out=dst[:, 1, :], in_=score[t][:].indirect(lists[lo][:]), func=COPY, scale=-1.0)
+                    nc.scalar.activation(out=score[t][:, cols], in_=acc[b], func=COPY)
 
-        def span(t):
+        def look_up(t, dst, hi, lo):
+            nc.scalar.activation(out=dst[:, 1, :], in_=score[t][:].indirect(lists[lo][:]), func=COPY, scale=-1.0)
+            if t == 0:
+                nc.vector.tensor_copy(out=dst[:, 0, :], in_=score[t][:].indirect(lists[hi][:]))
+            else:
+                nc.scalar.activation(out=dst[:, 0, :], in_=score[t][:].indirect(lists[hi][:]), func=COPY)
+
+        def high_low(t):
             nc.vector.tensor_tensor(out=ends[t][:], in0=first[t][:], in1=second[t][:], op=ALU.max)
+
+        def put_span(t):
             nc.vector.tensor_tensor(
                 out=span_at[:].indirect(lists["put"][:]), in0=ends[t][:, 0, :], in1=ends[t][:, 1, :], op=ALU.add
             )
@@ -133,59 +148,66 @@ def tile_attend_spanpassed_one_mixed_kernel(
             nc.vector.tensor_tensor(out=left[t][:], in0=score[t][:], in1=span_at[:], op=ALU.subtract)
 
         def pick(t):
-            nc.scalar.activation(out=picked[t][:], in_=left[t][:].indirect(lists["get"][:]), func=COPY)
+            nc.scalar.activation(out=picked[t], in_=left[t][:].indirect(lists["get"][:]), func=COPY)
 
         def add_low(t):
-            nc.vector.tensor_tensor(out=result[t][:], in0=picked[t][:], in1=ends[t][:, 1, :], op=ALU.subtract)
+            nc.vector.tensor_tensor(out=result[t][:], in0=picked[t], in1=ends[t][:, 1, :], op=ALU.subtract)
 
         def weigh(t, h, src):
-            nc.scalar.activation(out=weighted[h][:, :, t], in_=src, func=COPY, scale=row_factor[:, t : t + 1])
-
-        def weigh_both(t):
-            for h in range(2):
-                weigh(t, h, result[t][:, h * HALF : (h + 1) * HALF])
-
-        scores(0)
-        look_up(0)
-        span(0)
-        take_off(0)
-        scores(1)
-        look_up(1)
-        span(1)
-        take_off(1)
-        scores(2)
-        look_up(2)
-        pick(0)
-        span(2)
-        take_off(2)
-        add_low(0)
-        scores(3)
-        look_up(3)
-        pick(1)
-        add_low(1)
-        span(3)
-        pick(2)
-        weigh_both(0)
-        weigh_both(1)
-        add_low(2)
-        take_off(3)
-        weigh_both(2)
+            nc.scalar.activation(
+                out=pairs[h][:, t // 2, :, t % 2], in_=src, func=COPY, scale=row_factor[:, t : t + 1]
+            )
 
         last = PACK - 1
+        quantise_query(0)
+        acc = multiply(0)
+        quantise_query(1)
+        for t in range(PACK):
+            empty(t, acc)
+            look_up(t, first[t], "hi_a", "lo_a")
+            if t < last:
+                acc = multiply(t + 1)
+            look_up(t, second[t], "hi_b", "lo_b")
+            high_low(t)
+            if t == 0:
+                quantise_query(2)
+                quantise_query(3)
+            if t < last:
+                put_span(t)
+                take_off(t)
+        for t in range(last):
+            pick(t)
+        add_low(0)
+        put_span(last)
+        add_low(1)
+        add_low(2)
+        take_off(last)
+        for t in range(last):
+            for h in range(2):
+                weigh(t, h, result[t][:, h * HALF : (h + 1) * HALF])
+        last_picked = sb.tile([P, HALF], F32, name="last_picked")
+        nc.vector.tensor_tensor(
+            out=last_result[0][:],
+            in0=left[last][:].indirect(lists["get"][:, : HALF // 16]),
+            in1=ends[last][:, 1, :HALF],
+            op=ALU.subtract,
+        )
+        nc.scalar.activation(out=last_picked[:], in_=left[last][:].indirect(lists["get"][:, HALF // 16 :]), func=COPY)
+        nc.vector.tensor_tensor(out=last_result[1][:], in0=last_picked[:], in1=ends[last][:, 1, HALF:], op=ALU.subtract)
         for h in range(2):
-            nc.vector.tensor_tensor(
-                out=last_result[h][:],
-                in0=left[last][:].indirect(lists["get"][:, h * (HALF // 16) : (h + 1) * (HALF // 16)]),
-                in1=ends[last][:, 1, h * HALF : (h + 1) * HALF],
-                op=ALU.subtract,
-            )
             weigh(last, h, last_result[h][:])
+        mixed = []
         for h in range(2):
+            word = I32 if h == 0 else U32
+            words_in = pairs[h][:].rearrange("p u i e -> p u (i e)").bitcast(word).rearrange("p u i -> p i u")
+            words_out = weighted[h][:].bitcast(word).rearrange("p (i u) -> p i u", u=2)
+            if h == 0:
+                nc.vector.tensor_copy(out=words_out, in_=words_in)
+            else:
+                nc.scalar.copy(out=words_out, in_=words_in)
             codes = sb.tile([P, HALF], U32, name=f"w_codes{h}", align_bytes=64)
             scale = sb.tile([P, HALF], U8, name=f"w_scale{h}", align_bytes=64)
-            nc.vector.quantize_mx(
-                out=codes[:].bitcast(FP8X4), scales=scale[:], in_=weighted[h][:].rearrange("p i t -> p (i t)")
-            )
+            nc.vector.quantize_mx(out=codes[:].bitcast(FP8X4), scales=scale[:], in_=weighted[h][:])
             for c in range(E // P):
                 acc = ps.tile([P, HALF], F32, name=f"mixed{h}_{c}")
                 nc.tensor.matmul_mx(
@@ -197,11 +219,13 @@ def tile_attend_spanpassed_one_mixed_kernel(
                     start=True,
                     stop=True,
                 )
-                staged = sb.tile([P, HALF], F32, name=f"staged{h}_{c}")
-                rows_out = out[P * c : P * (c + 1), h * HALF : (h + 1) * HALF]
-                if c == 0:
-                    nc.vector.tensor_copy(out=staged[:], in_=acc[:])
-                    nc.sync.dma_start(out=rows_out, in_=staged[:])
-                else:
-                    nc.scalar.activation(out=staged[:], in_=acc[:], func=COPY)
-                    nc.scalar.dma_start(out=rows_out, in_=staged[:])
+                mixed.append((h, c, acc))
+        for h, c, acc in mixed:
+            staged = sb.tile([P, HALF], F32, name=f"staged{h}_{c}")
+            rows_out = out[P * c : P * (c + 1), h * HALF : (h + 1) * HALF]
+            if c == 0:
+                nc.vector.tensor_copy(out=staged[:], in_=acc[:])
+                nc.sync.dma_start(out=rows_out, in_=staged[:])
+            else:
+                nc.scalar.activation(out=staged[:], in_=acc[:], func=COPY)
+                nc.scalar.dma_start(out=rows_out, in_=staged[:])

@@ -38,16 +38,15 @@ def tile_attend_spanpassed_one_mixed_kernel(
 
         q_rows = query.rearrange("(p j) q -> p j q", j=PACK)
         q_raw = []
-        for h in range(2):
-            raw = sb.tile([P, PACK, Q // 2], F32, name=f"q_raw{h}")
-            nc.sync.dma_start(out=raw[:], in_=q_rows[:, :, h * (Q // 2) : (h + 1) * (Q // 2)])
+        for u in range(2):
+            raw = sb.tile([P, 2, Q], F32, name=f"q_raw{u}")
+            nc.sync.dma_start(out=raw[:], in_=q_rows[:, 2 * u : 2 * u + 2, :])
             q_raw.append(raw)
-            if h == 0:
-                for quad in range(4):
-                    nc.sync.dma_start(
-                        out=key_scale[32 * quad : 32 * quad + 4, :].bitcast(I32),
-                        in_=keys_scales[0, 4 * quad : 4 * quad + 4, :].bitcast(I32),
-                    )
+        for quad in range(4):
+            nc.sync.dma_start(
+                out=key_scale[32 * quad : 32 * quad + 4, :].bitcast(I32),
+                in_=keys_scales[0, 4 * quad : 4 * quad + 4, :].bitcast(I32),
+            )
         key_src = keys_words[0].rearrange("p n t -> p (n t)").bitcast(I32)
         key_words = []
         for b in range(T // BANK):
@@ -73,12 +72,12 @@ def tile_attend_spanpassed_one_mixed_kernel(
 
         q_first = sb.tile([P, P, PACK], BF16, name="q_first", align_bytes=64)
         q_rest = sb.tile([P, PACK - 1, P, PACK], BF16, name="q_rest", align_bytes=64)
-        for h in range(2):
-            cols = slice(h * (P // 2), (h + 1) * (P // 2))
-            dealt = q_raw[h][:].rearrange("p j (m t) -> p m t j", t=PACK)
-            nc.vector.tensor_copy(out=q_first[:, cols, :], in_=dealt[:, :, 0, :])
-            rest = q_rest[:, :, cols, :].rearrange("p t m j -> p m t j")
-            if h == 0:
+        for u in range(2):
+            places = slice(2 * u, 2 * u + 2)
+            dealt = q_raw[u][:].rearrange("p j (m t) -> p m t j", t=PACK)
+            nc.vector.tensor_copy(out=q_first[:, :, places], in_=dealt[:, :, 0, :])
+            rest = q_rest[:, :, :, places].rearrange("p t m j -> p m t j")
+            if u == 0:
                 nc.vector.tensor_copy(out=rest, in_=dealt[:, :, 1:PACK, :])
             else:
                 nc.scalar.activation(out=rest, in_=dealt[:, :, 1:PACK, :], func=COPY)
@@ -96,10 +95,9 @@ def tile_attend_spanpassed_one_mixed_kernel(
         second = [sb.tile([P, 2, I], F32, name=f"second{t}") for t in range(PACK)]
         ends = [sb.tile([P, 2, I], F32, name=f"ends{t}") for t in range(PACK)]
         left = [sb.tile([P, T], F32, name=f"left{t}") for t in range(PACK)]
-        result = [sb.tile([P, I], F32, name=f"result{t}") for t in range(PACK - 1)]
+        result = [ends[3][:, 0, :]] + [sb.tile([P, I], F32, name=f"result{t}")[:] for t in range(1, PACK - 1)]
         last_result = [sb.tile([P, HALF], F32, name=f"last_result{h}") for h in range(2)]
         pairs = [sb.tile([P, 2, HALF, 2], BF16, name=f"pairs{h}") for h in range(2)]
-        weighted = [sb.tile([P, HALF * PACK], BF16, name=f"weighted{h}", align_bytes=64) for h in range(2)]
         picked = [ends[2][:, 0, :], first[3][:, 0, :], second[3][:, 0, :]]
 
         def multiply(t):
@@ -151,7 +149,7 @@ def tile_attend_spanpassed_one_mixed_kernel(
             nc.scalar.activation(out=picked[t], in_=left[t][:].indirect(lists["get"][:]), func=COPY)
 
         def add_low(t):
-            nc.vector.tensor_tensor(out=result[t][:], in0=picked[t], in1=ends[t][:, 1, :], op=ALU.subtract)
+            nc.gpsimd.tensor_tensor(out=result[t], in0=picked[t], in1=ends[t][:, 1, :], op=ALU.subtract)
 
         def weigh(t, h, src):
             nc.scalar.activation(
@@ -177,39 +175,47 @@ def tile_attend_spanpassed_one_mixed_kernel(
                 take_off(t)
         for t in range(last):
             pick(t)
-        add_low(0)
-        put_span(last)
-        add_low(1)
-        add_low(2)
-        take_off(last)
+        last_span = sb.tile([P, I], F32, name="last_span")
+        nc.vector.tensor_tensor(out=last_span[:], in0=ends[last][:, 0, :], in1=ends[last][:, 1, :], op=ALU.add)
+        nc.vector.tensor_copy(out=span_at[:].indirect(lists["put"][:]), in_=last_span[:])
+        for t in range(last):
+            add_low(t)
+        for b in range(T // BANK):
+            cols = slice(b * BANK, (b + 1) * BANK)
+            nc.vector.tensor_tensor(out=left[last][:, cols], in0=acc[b], in1=span_at[:, cols], op=ALU.subtract)
         for t in range(last):
             for h in range(2):
                 weigh(t, h, result[t][:, h * HALF : (h + 1) * HALF])
-        last_picked = sb.tile([P, HALF], F32, name="last_picked")
-        nc.vector.tensor_tensor(
-            out=last_result[0][:],
-            in0=left[last][:].indirect(lists["get"][:, : HALF // 16]),
-            in1=ends[last][:, 1, :HALF],
-            op=ALU.subtract,
-        )
-        nc.scalar.activation(out=last_picked[:], in_=left[last][:].indirect(lists["get"][:, HALF // 16 :]), func=COPY)
-        nc.vector.tensor_tensor(out=last_result[1][:], in0=last_picked[:], in1=ends[last][:, 1, HALF:], op=ALU.subtract)
         for h in range(2):
-            weigh(last, h, last_result[h][:])
+            nc.vector.tensor_tensor(
+                out=last_result[h][:],
+                in0=left[last][:].indirect(lists["get"][:, h * (HALF // 16) : (h + 1) * (HALF // 16)]),
+                in1=ends[last][:, 1, h * HALF : (h + 1) * HALF],
+                op=ALU.subtract,
+            )
+        pieces = ((0, 0, HALF), (1, 0, HALF // 2), (1, HALF // 2, HALF // 2))
+        for h, lo, n in pieces:
+            nc.scalar.activation(
+                out=pairs[h][:, last // 2, lo : lo + n, last % 2],
+                in_=last_result[h][:, lo : lo + n],
+                func=COPY,
+                scale=row_factor[:, last : last + 1],
+            )
         mixed = []
-        for h in range(2):
+        for h, lo, n in pieces:
             word = I32 if h == 0 else U32
-            words_in = pairs[h][:].rearrange("p u i e -> p u (i e)").bitcast(word).rearrange("p u i -> p i u")
-            words_out = weighted[h][:].bitcast(word).rearrange("p (i u) -> p i u", u=2)
+            weighted = sb.tile([P, n * PACK], BF16, name=f"weighted{h}_{lo}", align_bytes=64)
+            words_in = pairs[h][:, :, lo : lo + n, :].rearrange("p u i e -> p u (i e)").bitcast(word).rearrange("p u i -> p i u")
+            words_out = weighted[:].bitcast(word).rearrange("p (i u) -> p i u", u=2)
             if h == 0:
                 nc.vector.tensor_copy(out=words_out, in_=words_in)
             else:
                 nc.scalar.copy(out=words_out, in_=words_in)
-            codes = sb.tile([P, HALF], U32, name=f"w_codes{h}", align_bytes=64)
-            scale = sb.tile([P, HALF], U8, name=f"w_scale{h}", align_bytes=64)
-            nc.vector.quantize_mx(out=codes[:].bitcast(FP8X4), scales=scale[:], in_=weighted[h][:])
+            codes = sb.tile([P, n], U32, name=f"w_codes{h}_{lo}", align_bytes=64)
+            scale = sb.tile([P, n], U8, name=f"w_scale{h}_{lo}", align_bytes=64)
+            nc.vector.quantize_mx(out=codes[:].bitcast(FP8X4), scales=scale[:], in_=weighted[:])
             for c in range(E // P):
-                acc = ps.tile([P, HALF], F32, name=f"mixed{h}_{c}")
+                acc = ps.tile([P, n], F32, name=f"mixed{h}_{lo}_{c}")
                 nc.tensor.matmul_mx(
                     out=acc[:],
                     lhsT=mix_codes[:, 2 * P * c : 2 * P * (c + 1)].bitcast(FP4X4),
@@ -219,10 +225,10 @@ def tile_attend_spanpassed_one_mixed_kernel(
                     start=True,
                     stop=True,
                 )
-                mixed.append((h, c, acc))
-        for h, c, acc in mixed:
-            staged = sb.tile([P, HALF], F32, name=f"staged{h}_{c}")
-            rows_out = out[P * c : P * (c + 1), h * HALF : (h + 1) * HALF]
+                mixed.append((h * HALF + lo, n, c, acc))
+        for lo, n, c, acc in mixed:
+            staged = sb.tile([P, n], F32, name=f"staged{lo}_{c}")
+            rows_out = out[P * c : P * (c + 1), lo : lo + n]
             if c == 0:
                 nc.vector.tensor_copy(out=staged[:], in_=acc[:])
                 nc.sync.dma_start(out=rows_out, in_=staged[:])

@@ -19,6 +19,7 @@ COPY = mybir.ActivationFunctionType.Copy
 P = 128
 PACK = 4
 BANK = 512
+BANK_BYTES = 4 * BANK
 HALF = I // 2
 
 
@@ -29,7 +30,6 @@ def tile_attend_spanpassed_one_mixed_kernel(
     with ExitStack() as ctx:
         sb = ctx.enter_context(tc.tile_pool(name="sb", bufs=1))
         ps = ctx.enter_context(tc.psum_pool(name="ps", bufs=1))
-        score_ps = ctx.enter_context(tc.psum_pool(name="score_ps", bufs=1))
 
         key_scale = sb.tile([P, T], U8, name="key_scale", align_bytes=64)
         mix_scale = sb.tile([P, E], U8, name="mix_scale", align_bytes=64)
@@ -67,8 +67,9 @@ def tile_attend_spanpassed_one_mixed_kernel(
                 in_=mix_scales[0, 4 * quad : 4 * quad + 4, :].bitcast(I32),
             )
 
-        span_at = sb.tile([P, T], F32, name="span_at")
-        nc.vector.memset(span_at[:], 0.0)
+        span_at = [sb.tile([P, T], F32, name=f"span_at{n}") for n in range(2)]
+        for window in span_at:
+            nc.vector.memset(window[:], 0.0)
 
         q_first = sb.tile([P, P, PACK], BF16, name="q_first", align_bytes=64)
         q_rest = sb.tile([P, PACK - 1, P, PACK], BF16, name="q_rest", align_bytes=64)
@@ -91,59 +92,67 @@ def tile_attend_spanpassed_one_mixed_kernel(
             )
 
         score = [sb.tile([P, T], F32, name=f"score{t}") for t in range(PACK)]
-        first = [sb.tile([P, 2, I], F32, name=f"first{t}") for t in range(PACK)]
-        second = [sb.tile([P, 2, I], F32, name=f"second{t}") for t in range(PACK)]
+        highs = [sb.tile([P, 2 * I], F32, name=f"highs{t}") for t in range(PACK)]
+        lows = [sb.tile([P, 2 * I], F32, name=f"lows{t}") for t in range(PACK)]
         ends = [sb.tile([P, 2, I], F32, name=f"ends{t}") for t in range(PACK)]
-        left = [sb.tile([P, T], F32, name=f"left{t}") for t in range(PACK)]
+        left = [highs[1], highs[2]] + [sb.tile([P, T], F32, name=f"left{t}") for t in range(2, PACK)]
         result = [ends[3][:, 0, :]] + [sb.tile([P, I], F32, name=f"result{t}")[:] for t in range(1, PACK - 1)]
         last_result = [sb.tile([P, HALF], F32, name=f"last_result{h}") for h in range(2)]
         pairs = [sb.tile([P, 2, HALF, 2], BF16, name=f"pairs{h}") for h in range(2)]
-        picked = [ends[2][:, 0, :], first[3][:, 0, :], second[3][:, 0, :]]
+        picked = [ends[2][:, 0, :], lows[3][:, :I], lows[3][:, I:]]
+
+        mix_banks = [ps.tile([P, HALF], F32, name=f"mix_bank{n}", offset=BANK_BYTES * (2 + n)) for n in range(6)]
 
         def multiply(t):
+            width = BANK // 2 if t == 0 else BANK
             if t == 0:
-                acc = [score_ps.tile([P, BANK], F32, name=f"first_acc{b}", offset=4 * BANK * b)[:] for b in range(T // BANK)]
+                acc = [ps.tile([P, width], F32, name=f"first_acc{b}", offset=BANK_BYTES * b)[:] for b in range(2)]
+                acc = acc + [bank[:] for bank in mix_banks[:2]]
             else:
-                both = score_ps.tile([P, T], F32, name=f"acc{t}", tag="acc", offset=0)
-                acc = [both[:, b * BANK : (b + 1) * BANK] for b in range(T // BANK)]
-            for b in range(T // BANK):
-                cols = slice(b * BANK, (b + 1) * BANK)
+                both = ps.tile([P, T], F32, name=f"acc{t}", tag="acc", offset=0)
+                acc = [both[:, b * width : (b + 1) * width] for b in range(T // width)]
+            for b, dst in enumerate(acc):
+                lo = b * width
                 nc.tensor.matmul_mx(
-                    out=acc[b],
+                    out=dst,
                     lhsT=q_codes[t][:].bitcast(FP8X4),
                     lhsT_scale=q_scale[t][:],
-                    rhs=key_words[b][:].bitcast(FP8X4),
-                    rhs_scale=key_scale[:, cols],
+                    rhs=key_words[lo // BANK][:, lo % BANK : lo % BANK + width].bitcast(FP8X4),
+                    rhs_scale=key_scale[:, lo : lo + width],
                     start=True,
                     stop=True,
                 )
             return acc
 
         def empty(t, acc):
-            for b in range(T // BANK):
-                cols = slice(b * BANK, (b + 1) * BANK)
-                if t == 0 and b == 1:
-                    nc.vector.tensor_copy(out=score[t][:, cols], in_=acc[b])
+            width = T // len(acc)
+            for b, src in enumerate(acc):
+                dst = score[t][:, b * width : (b + 1) * width]
+                if t == 0 and b % 2 == 1:
+                    nc.vector.tensor_copy(out=dst, in_=src)
                 else:
-                    nc.scalar.activation(out=score[t][:, cols], in_=acc[b], func=COPY)
+                    nc.scalar.activation(out=dst, in_=src, func=COPY)
 
-        def look_up(t, dst, hi, lo):
-            nc.scalar.activation(out=dst[:, 1, :], in_=score[t][:].indirect(lists[lo][:]), func=COPY, scale=-1.0)
-            if t == 0:
-                nc.vector.tensor_copy(out=dst[:, 0, :], in_=score[t][:].indirect(lists[hi][:]))
+        def look_up(t, name, on_vector):
+            window = score[t][:].indirect(lists[name][:])
+            cols = slice(0, I) if name in ("hi_a", "lo_a") else slice(I, 2 * I)
+            if on_vector:
+                nc.vector.tensor_copy(out=highs[t][:, cols], in_=window)
+            elif name in ("hi_a", "hi_b"):
+                nc.scalar.activation(out=highs[t][:, cols], in_=window, func=COPY)
             else:
-                nc.scalar.activation(out=dst[:, 0, :], in_=score[t][:].indirect(lists[hi][:]), func=COPY)
+                nc.scalar.activation(out=lows[t][:, cols], in_=window, func=COPY, scale=-1.0)
 
-        def high_low(t):
-            nc.vector.tensor_tensor(out=ends[t][:], in0=first[t][:], in1=second[t][:], op=ALU.max)
+        def higher(t, side, pair):
+            nc.vector.tensor_tensor(out=ends[t][:, side, :], in0=pair[:, :I], in1=pair[:, I:], op=ALU.max)
 
         def put_span(t):
             nc.vector.tensor_tensor(
-                out=span_at[:].indirect(lists["put"][:]), in0=ends[t][:, 0, :], in1=ends[t][:, 1, :], op=ALU.add
+                out=span_at[t % 2][:].indirect(lists["put"][:]), in0=ends[t][:, 0, :], in1=ends[t][:, 1, :], op=ALU.add
             )
 
         def take_off(t):
-            nc.vector.tensor_tensor(out=left[t][:], in0=score[t][:], in1=span_at[:], op=ALU.subtract)
+            nc.vector.tensor_tensor(out=left[t][:], in0=score[t][:], in1=span_at[t % 2][:], op=ALU.subtract)
 
         def pick(t):
             nc.scalar.activation(out=picked[t], in_=left[t][:].indirect(lists["get"][:]), func=COPY)
@@ -162,27 +171,36 @@ def tile_attend_spanpassed_one_mixed_kernel(
         quantise_query(1)
         for t in range(PACK):
             empty(t, acc)
-            look_up(t, first[t], "hi_a", "lo_a")
+            if t <= 1:
+                look_up(t, "hi_a", True)
+            if t > 0:
+                put_span(t - 1)
+            if t == last:
+                take_off(t - 1)
+            look_up(t, "lo_a", False)
             if t < last:
                 acc = multiply(t + 1)
-            look_up(t, second[t], "hi_b", "lo_b")
-            high_low(t)
+            if t > 1:
+                look_up(t, "hi_a", False)
+            look_up(t, "hi_b", t == 0)
+            look_up(t, "lo_b", False)
+            higher(t, 0, highs[t])
+            higher(t, 1, lows[t])
             if t == 0:
                 quantise_query(2)
                 quantise_query(3)
-            if t < last:
-                put_span(t)
-                take_off(t)
+            elif t < last:
+                take_off(t - 1)
         for t in range(last):
             pick(t)
         last_span = sb.tile([P, I], F32, name="last_span")
         nc.vector.tensor_tensor(out=last_span[:], in0=ends[last][:, 0, :], in1=ends[last][:, 1, :], op=ALU.add)
-        nc.vector.tensor_copy(out=span_at[:].indirect(lists["put"][:]), in_=last_span[:])
+        nc.vector.tensor_copy(out=span_at[last % 2][:].indirect(lists["put"][:]), in_=last_span[:])
         for t in range(last):
             add_low(t)
         for b in range(T // BANK):
             cols = slice(b * BANK, (b + 1) * BANK)
-            nc.vector.tensor_tensor(out=left[last][:, cols], in0=acc[b], in1=span_at[:, cols], op=ALU.subtract)
+            nc.vector.tensor_tensor(out=left[last][:, cols], in0=acc[b], in1=span_at[last % 2][:, cols], op=ALU.subtract)
         for t in range(last):
             for h in range(2):
                 weigh(t, h, result[t][:, h * HALF : (h + 1) * HALF])
@@ -215,9 +233,9 @@ def tile_attend_spanpassed_one_mixed_kernel(
             scale = sb.tile([P, n], U8, name=f"w_scale{h}_{lo}", align_bytes=64)
             nc.vector.quantize_mx(out=codes[:].bitcast(FP8X4), scales=scale[:], in_=weighted[:])
             for c in range(E // P):
-                acc = ps.tile([P, n], F32, name=f"mixed{h}_{lo}_{c}")
+                acc = mix_banks[len(mixed)][:, :n]
                 nc.tensor.matmul_mx(
-                    out=acc[:],
+                    out=acc,
                     lhsT=mix_codes[:, 2 * P * c : 2 * P * (c + 1)].bitcast(FP4X4),
                     lhsT_scale=mix_scale[:, P * c : P * (c + 1)],
                     rhs=codes[:].bitcast(FP8X4),
@@ -230,8 +248,8 @@ def tile_attend_spanpassed_one_mixed_kernel(
             staged = sb.tile([P, n], F32, name=f"staged{lo}_{c}")
             rows_out = out[P * c : P * (c + 1), lo : lo + n]
             if c == 0:
-                nc.vector.tensor_copy(out=staged[:], in_=acc[:])
+                nc.vector.tensor_copy(out=staged[:], in_=acc)
                 nc.sync.dma_start(out=rows_out, in_=staged[:])
             else:
-                nc.scalar.activation(out=staged[:], in_=acc[:], func=COPY)
+                nc.scalar.activation(out=staged[:], in_=acc, func=COPY)
                 nc.scalar.dma_start(out=rows_out, in_=staged[:])

from contextlib import ExitStack

import concourse.mybir as mybir

D, T, I, Q, E = 512, 1024, 512, 512, 256
FLOPS = 2 * D * Q * T + 2 * Q * E * I

F32 = mybir.dt.float32
BF16 = mybir.dt.bfloat16
I32 = mybir.dt.int32
U32 = mybir.dt.uint32
U16 = mybir.dt.uint16
U8 = mybir.dt.uint8
FP8X4 = mybir.dt.float8_e4m3fn_x4
FP4X4 = mybir.dt.float4_e2m1fn_x4
ALU = mybir.AluOpType
COPY = mybir.ActivationFunctionType.Copy

P = 128
PACK = 4
BANK = 512
BANK_BYTES = 4 * BANK
HALF = I // 2


def tile_attend_spanpassed_one_mixed_kernel(
    tc, query, keys_words, keys_scales, rowf, mix_words, mix_scales, offs, offs2, offs3, offs4, offs5, offs6, out
):
    nc = tc.nc
    with ExitStack() as ctx:
        sb = ctx.enter_context(tc.tile_pool(name="sb", bufs=1))
        ps = ctx.enter_context(tc.psum_pool(name="ps", bufs=1))

        key_scale = sb.tile([P, T], U8, name="key_scale", align_bytes=64)
        mix_scale = sb.tile([P, E], U8, name="mix_scale", align_bytes=64)
        nc.vector.memset(key_scale[:].bitcast(I32), 0)
        nc.vector.memset(mix_scale[:].bitcast(I32), 0)

        q_rows = query.rearrange("(p j) q -> p j q", j=PACK)
        q_raw = []
        for u in range(2):
            raw = sb.tile([P, 2, Q], F32, name=f"q_raw{u}")
            nc.sync.dma_start(out=raw[:], in_=q_rows[:, 2 * u : 2 * u + 2, :])
            q_raw.append(raw)
        for quad in range(4):
            nc.sync.dma_start(
                out=key_scale[32 * quad : 32 * quad + 4, :].bitcast(I32),
                in_=keys_scales[0, 4 * quad : 4 * quad + 4, :].bitcast(I32),
            )
        key_src = keys_words[0].rearrange("p n t -> p (n t)").bitcast(I32)
        key_words = []
        for b in range(T // BANK):
            words = sb.tile([P, BANK], I32, name=f"key_words{b}", align_bytes=64)
            nc.sync.dma_start(out=words[:], in_=key_src[:, b * BANK : (b + 1) * BANK])
            key_words.append(words)
        lists = {}
        for name, src in (("lo_a", offs3), ("hi_a", offs), ("lo_b", offs4), ("hi_b", offs2), ("put", offs5), ("get", offs6)):
            lists[name] = sb.tile([P, I // 16], U16, name=f"list_{name}")
            nc.sync.dma_start(lists[name][:], src)
        row_factor = sb.tile([P, PACK], F32, name="row_factor")
        nc.sync.dma_start(out=row_factor[:], in_=rowf.rearrange("(p t) o -> p (t o)", t=PACK))
        mix_codes = sb.tile([P, 2 * E], U8, name="mix_codes", align_bytes=64)
        nc.sync.dma_start(out=mix_codes[:].bitcast(I32), in_=mix_words[0].bitcast(I32))
        for quad in range(4):
            nc.sync.dma_start(
                out=mix_scale[32 * quad : 32 * quad + 4, :].bitcast(I32),
                in_=mix_scales[0, 4 * quad : 4 * quad + 4, :].bitcast(I32),
            )

        span_at = [sb.tile([P, T], F32, name=f"span_at{n}") for n in range(2)]
        for window in span_at:
            nc.vector.memset(window[:], 0.0)

        q_first = sb.tile([P, P, PACK], BF16, name="q_first", align_bytes=64)
        q_rest = sb.tile([P, PACK - 1, P, PACK], BF16, name="q_rest", align_bytes=64)
        for u in range(2):
            places = slice(2 * u, 2 * u + 2)
            dealt = q_raw[u][:].rearrange("p j (m t) -> p m t j", t=PACK)
            nc.vector.tensor_copy(out=q_first[:, :, places], in_=dealt[:, :, 0, :])
            rest = q_rest[:, :, :, places].rearrange("p t m j -> p m t j")
            if u == 0:
                nc.vector.tensor_copy(out=rest, in_=dealt[:, :, 1:PACK, :])
            else:
                nc.scalar.activation(out=rest, in_=dealt[:, :, 1:PACK, :], func=COPY)
        q_codes = [sb.tile([P, P], U32, name=f"q_codes{t}", align_bytes=64) for t in range(PACK)]
        q_scale = [sb.tile([P, P], U8, name=f"q_scale{t}", align_bytes=64) for t in range(PACK)]

        def quantise_query(t):
            src = q_first[:] if t == 0 else q_rest[:, t - 1, :, :]
            nc.vector.quantize_mx(
                out=q_codes[t][:].bitcast(FP8X4), scales=q_scale[t][:], in_=src.rearrange("p m j -> p (m j)")
            )

        score = [sb.tile([P, T], F32, name=f"score{t}") for t in range(PACK)]
        highs = [sb.tile([P, 2 * I], F32, name=f"highs{t}") for t in range(PACK)]
        lows = [sb.tile([P, 2 * I], F32, name=f"lows{t}") for t in range(PACK)]
        ends = [sb.tile([P, 2, I], F32, name=f"ends{t}") for t in range(PACK)]
        left = [highs[1], highs[2]] + [sb.tile([P, T], F32, name=f"left{t}") for t in range(2, PACK)]
        result = [ends[3][:, 0, :]] + [sb.tile([P, I], F32, name=f"result{t}")[:] for t in range(1, PACK - 1)]
        last_result = [sb.tile([P, HALF], F32, name=f"last_result{h}") for h in range(2)]
        pairs = [sb.tile([P, 2, HALF, 2], BF16, name=f"pairs{h}") for h in range(2)]
        picked = [ends[2][:, 0, :], lows[3][:, :I], lows[3][:, I:]]

        mix_banks = [ps.tile([P, HALF], F32, name=f"mix_bank{n}", offset=BANK_BYTES * (2 + n)) for n in range(6)]

        def multiply(t):
            width = BANK // 2 if t == 0 else BANK
            if t == 0:
                acc = [ps.tile([P, width], F32, name=f"first_acc{b}", offset=BANK_BYTES * b)[:] for b in range(2)]
                acc = acc + [bank[:] for bank in mix_banks[:2]]
            else:
                both = ps.tile([P, T], F32, name=f"acc{t}", tag="acc", offset=0)
                acc = [both[:, b * width : (b + 1) * width] for b in range(T // width)]
            for b, dst in enumerate(acc):
                lo = b * width
                nc.tensor.matmul_mx(
                    out=dst,
                    lhsT=q_codes[t][:].bitcast(FP8X4),
                    lhsT_scale=q_scale[t][:],
                    rhs=key_words[lo // BANK][:, lo % BANK : lo % BANK + width].bitcast(FP8X4),
                    rhs_scale=key_scale[:, lo : lo + width],
                    start=True,
                    stop=True,
                )
            return acc

        def empty(t, acc):
            width = T // len(acc)
            for b, src in enumerate(acc):
                dst = score[t][:, b * width : (b + 1) * width]
                if t == 0 and b % 2 == 1:
                    nc.vector.tensor_copy(out=dst, in_=src)
                else:
                    nc.scalar.activation(out=dst, in_=src, func=COPY)

        def look_up(t, name, on_vector):
            window = score[t][:].indirect(lists[name][:])
            cols = slice(0, I) if name in ("hi_a", "lo_a") else slice(I, 2 * I)
            if on_vector:
                nc.vector.tensor_copy(out=highs[t][:, cols], in_=window)
            elif name in ("hi_a", "hi_b"):
                nc.scalar.activation(out=highs[t][:, cols], in_=window, func=COPY)
            else:
                nc.scalar.activation(out=lows[t][:, cols], in_=window, func=COPY, scale=-1.0)

        def higher(t, side, pair):
            nc.vector.tensor_tensor(out=ends[t][:, side, :], in0=pair[:, :I], in1=pair[:, I:], op=ALU.max)

        def put_span(t):
            nc.vector.tensor_tensor(
                out=span_at[t % 2][:].indirect(lists["put"][:]), in0=ends[t][:, 0, :], in1=ends[t][:, 1, :], op=ALU.add
            )

        def take_off(t):
            nc.vector.tensor_tensor(out=left[t][:], in0=score[t][:], in1=span_at[t % 2][:], op=ALU.subtract)

        def pick(t):
            nc.scalar.activation(out=picked[t], in_=left[t][:].indirect(lists["get"][:]), func=COPY)

        def add_low(t):
            nc.gpsimd.tensor_tensor(out=result[t], in0=picked[t], in1=ends[t][:, 1, :], op=ALU.subtract)

        def weigh(t, h, src):
            nc.scalar.activation(
                out=pairs[h][:, t // 2, :, t % 2], in_=src, func=COPY, scale=row_factor[:, t : t + 1]
            )

        last = PACK - 1
        quantise_query(0)
        acc = multiply(0)
        quantise_query(1)
        for t in range(PACK):
            empty(t, acc)
            if t <= 1:
                look_up(t, "hi_a", True)
            if t > 0:
                put_span(t - 1)
            if t == last:
                take_off(t - 1)
            look_up(t, "lo_a", False)
            if t < last:
                acc = multiply(t + 1)
            if t > 1:
                look_up(t, "hi_a", False)
            look_up(t, "hi_b", t == 0)
            look_up(t, "lo_b", False)
            higher(t, 0, highs[t])
            higher(t, 1, lows[t])
            if t == 0:
                quantise_query(2)
                quantise_query(3)
            elif t < last:
                take_off(t - 1)
        for t in range(last):
            pick(t)
        last_span = sb.tile([P, I], F32, name="last_span")
        nc.vector.tensor_tensor(out=last_span[:], in0=ends[last][:, 0, :], in1=ends[last][:, 1, :], op=ALU.add)
        nc.vector.tensor_copy(out=span_at[last % 2][:].indirect(lists["put"][:]), in_=last_span[:])
        for t in range(last):
            add_low(t)
        for b in range(T // BANK):
            cols = slice(b * BANK, (b + 1) * BANK)
            nc.vector.tensor_tensor(out=left[last][:, cols], in0=acc[b], in1=span_at[last % 2][:, cols], op=ALU.subtract)
        for t in range(last):
            for h in range(2):
                weigh(t, h, result[t][:, h * HALF : (h + 1) * HALF])
        for h in range(2):
            nc.vector.tensor_tensor(
                out=last_result[h][:],
                in0=left[last][:].indirect(lists["get"][:, h * (HALF // 16) : (h + 1) * (HALF // 16)]),
                in1=ends[last][:, 1, h * HALF : (h + 1) * HALF],
                op=ALU.subtract,
            )
        pieces = ((0, 0, HALF), (1, 0, HALF // 2), (1, HALF // 2, HALF // 2))
        for h, lo, n in pieces:
            nc.scalar.activation(
                out=pairs[h][:, last // 2, lo : lo + n, last % 2],
                in_=last_result[h][:, lo : lo + n],
                func=COPY,
                scale=row_factor[:, last : last + 1],
            )
        mixed = []
        for h, lo, n in pieces:
            word = I32 if h == 0 else U32
            weighted = sb.tile([P, n * PACK], BF16, name=f"weighted{h}_{lo}", align_bytes=64)
            words_in = pairs[h][:, :, lo : lo + n, :].rearrange("p u i e -> p u (i e)").bitcast(word).rearrange("p u i -> p i u")
            words_out = weighted[:].bitcast(word).rearrange("p (i u) -> p i u", u=2)
            if h == 0:
                nc.vector.tensor_copy(out=words_out, in_=words_in)
            else:
                nc.scalar.copy(out=words_out, in_=words_in)
            codes = sb.tile([P, n], U32, name=f"w_codes{h}_{lo}", align_bytes=64)
            scale = sb.tile([P, n], U8, name=f"w_scale{h}_{lo}", align_bytes=64)
            nc.vector.quantize_mx(out=codes[:].bitcast(FP8X4), scales=scale[:], in_=weighted[:])
            for c in range(E // P):
                acc = mix_banks[len(mixed)][:, :n]
                nc.tensor.matmul_mx(
                    out=acc,
                    lhsT=mix_codes[:, 2 * P * c : 2 * P * (c + 1)].bitcast(FP4X4),
                    lhsT_scale=mix_scale[:, P * c : P * (c + 1)],
                    rhs=codes[:].bitcast(FP8X4),
                    rhs_scale=scale[:],
                    start=True,
                    stop=True,
                )
                mixed.append((h * HALF + lo, n, c, acc))
        for lo, n, c, acc in mixed:
            staged = sb.tile([P, n], F32, name=f"staged{lo}_{c}")
            rows_out = out[P * c : P * (c + 1), lo : lo + n]
            if c == 0:
                nc.vector.tensor_copy(out=staged[:], in_=acc)
                nc.sync.dma_start(out=rows_out, in_=staged[:])
            else:
                nc.scalar.activation(out=staged[:], in_=acc, func=COPY)
                nc.scalar.dma_start(out=rows_out, in_=staged[:])
